import numpy as np
import ml_dtypes

BF16 = ml_dtypes.bfloat16


def bf(x):
    return np.asarray(x, np.float32).astype(BF16)


def f32(x):
    return np.asarray(x, np.float32)


def f64(x):
    return np.asarray(x).astype(np.float64)


def striped(idx):
    return np.tile(idx.reshape(-1, 16).T, (8, 1))


S, K, M, N = 1024, 256, 512, 256


def gelu_tanh(v):
    return 0.5 * v * (1.0 + np.tanh(np.sqrt(2.0 / np.pi) * (v + 0.044715 * v**3)))


def setup_inputs():
    return {"table": bf(np.random.standard_normal((K, S))), "w": bf(np.random.standard_normal((K, M)) / np.sqrt(K)), "b": f32(0.5 * np.random.standard_normal((M, 1))), "offs": striped(np.random.permutation(np.tile(np.arange(S), 2))[:N])}


def reference(table, w, b, offs):
    idx = offs[:16].T.reshape(-1)
    x = f64(table)[:, idx]
    y = f64(w).T @ x
    return gelu_tanh(y + f64(b))

@@ -1,0 +1,55 @@
+import concourse.mybir as mybir
+
+P = 128
+K = 256
+S = 1024
+M = 512
+N = 256
+K_BLOCKS = K // P
+M_BLOCKS = M // P
+
+FLOPS = 2 * K * M * N
+
+BF16 = mybir.dt.bfloat16
+F32 = mybir.dt.float32
+U16 = mybir.dt.uint16
+GELU = mybir.ActivationFunctionType.Gelu_apprx_tanh
+
+
+def tile_gather_matmul_kernel(tc, table, w, b, offs, out):
+    nc = tc.nc
+    with (
+        tc.tile_pool(name="held", bufs=1) as held,
+        tc.tile_pool(name="staged", bufs=M_BLOCKS) as staged,
+        tc.psum_pool(name="psum", bufs=M_BLOCKS) as psum,
+    ):
+        offsets = held.tile([P, N // 16], U16, name="offsets")
+        nc.sync.dma_start(offsets[:], offs)
+
+        table_blocks = []
+        weight_blocks = []
+        for k in range(K_BLOCKS):
+            table_block = held.tile([P, S], BF16, name=f"table{k}")
+            nc.sync.dma_start(table_block[:], table[k * P : (k + 1) * P, :])
+            table_blocks.append(table_block)
+            weight_block = held.tile([P, M], BF16, name=f"weights{k}")
+            nc.scalar.dma_start(weight_block[:], w[k * P : (k + 1) * P, :])
+            weight_blocks.append(weight_block)
+
+        bias = held.tile([P, M_BLOCKS], F32, name="bias")
+        with nc.allow_non_contiguous_dma(reason="512 bias values, one to a partition"):
+            nc.scalar.dma_start(bias[:], b.rearrange("(a p) o -> p (a o)", p=P))
+
+        for m in range(M_BLOCKS):
+            bank = psum.tile([P, N], F32, name="bank")
+            for k in range(K_BLOCKS):
+                nc.tensor.matmul(
+                    bank[:],
+                    weight_blocks[k][:, m * P : (m + 1) * P],
+                    table_blocks[k][:].indirect(offsets[:]),
+                    start=(k == 0),
+                    stop=(k == K_BLOCKS - 1),
+                )
+            result = staged.tile([P, N], F32, name="result")
+            nc.scalar.activation(result[:], bank[:], GELU, bias=bias[:, m : m + 1])
+            nc.sync.dma_start(out[m * P : (m + 1) * P, :], result[:])

@@ -21,7 +21,7 @@ def tile_gather_matmul_kernel(tc, table, w, b, offs, out):
     with (
         tc.tile_pool(name="held", bufs=1) as held,
         tc.tile_pool(name="staged", bufs=M_BLOCKS) as staged,
-        tc.psum_pool(name="psum", bufs=M_BLOCKS) as psum,
+        tc.psum_pool(name="psum", bufs=1) as psum,
     ):
         offsets = held.tile([P, N // 16], U16, name="offsets")
         nc.sync.dma_start(offsets[:], offs)
@@ -38,18 +38,25 @@ def tile_gather_matmul_kernel(tc, table, w, b, offs, out):
 
         bias = held.tile([P, M_BLOCKS], F32, name="bias")
         with nc.allow_non_contiguous_dma(reason="512 bias values, one to a partition"):
-            nc.scalar.dma_start(bias[:], b.rearrange("(a p) o -> p (a o)", p=P))
+            nc.gpsimd.dma_start(bias[:], b.rearrange("(a p) o -> p (a o)", p=P))
 
-        for m in range(M_BLOCKS):
-            bank = psum.tile([P, N], F32, name="bank")
-            for k in range(K_BLOCKS):
+        zeros = held.tile([P, 1], F32, name="zeros")
+        nc.vector.memset(zeros[:], 0.0)
+        unused = held.tile([P, 1], F32, name="unused")
+        nc.scalar.activation(unused[:], zeros[:], GELU)
+
+        banks = [psum.tile([P, N], F32, name=f"bank{m}") for m in range(M_BLOCKS)]
+        for k in range(K_BLOCKS):
+            for m in range(M_BLOCKS):
                 nc.tensor.matmul(
-                    bank[:],
+                    banks[m][:],
                     weight_blocks[k][:, m * P : (m + 1) * P],
                     table_blocks[k][:].indirect(offsets[:]),
                     start=(k == 0),
                     stop=(k == K_BLOCKS - 1),
                 )
+
+        for m in range(M_BLOCKS):
             result = staged.tile([P, N], F32, name="result")
-            nc.scalar.activation(result[:], bank[:], GELU, bias=bias[:, m : m + 1])
+            nc.scalar.activation(result[:], banks[m][:], GELU, bias=bias[:, m : m + 1])
             nc.sync.dma_start(out[m * P : (m + 1) * P, :], result[:])

@@ -14,6 +14,8 @@ BF16 = mybir.dt.bfloat16
 F32 = mybir.dt.float32
 U16 = mybir.dt.uint16
 GELU = mybir.ActivationFunctionType.Gelu_apprx_tanh
+WARM_MATMULS = 6
+WARM_COLUMNS = 512
 
 
 def tile_gather_matmul_kernel(tc, table, w, b, offs, out):
@@ -38,12 +40,18 @@ def tile_gather_matmul_kernel(tc, table, w, b, offs, out):
 
         bias = held.tile([P, M_BLOCKS], F32, name="bias")
         with nc.allow_non_contiguous_dma(reason="512 bias values, one to a partition"):
-            nc.gpsimd.dma_start(bias[:], b.rearrange("(a p) o -> p (a o)", p=P))
+            nc.scalar.dma_start(bias[:], b.rearrange("(a p) o -> p (a o)", p=P))
 
         zeros = held.tile([P, 1], F32, name="zeros")
         nc.vector.memset(zeros[:], 0.0)
         unused = held.tile([P, 1], F32, name="unused")
         nc.scalar.activation(unused[:], zeros[:], GELU)
+
+        warm_in = held.tile([P, WARM_COLUMNS], BF16, name="warm_in")
+        nc.vector.memset(warm_in[:], 0.0)
+        warm_bank = psum.tile([P, WARM_COLUMNS], F32, name="warm_bank")
+        for i in range(WARM_MATMULS):
+            nc.tensor.matmul(warm_bank[:], warm_in[:, 0:P], warm_in[:], start=True, stop=True)
 
         banks = [psum.tile([P, N], F32, name=f"bank{m}") for m in range(M_BLOCKS)]
         for k in range(K_BLOCKS):

@@ -14,8 +14,6 @@ BF16 = mybir.dt.bfloat16
 F32 = mybir.dt.float32
 U16 = mybir.dt.uint16
 GELU = mybir.ActivationFunctionType.Gelu_apprx_tanh
-WARM_MATMULS = 6
-WARM_COLUMNS = 512
 
 
 def tile_gather_matmul_kernel(tc, table, w, b, offs, out):
@@ -28,30 +26,20 @@ def tile_gather_matmul_kernel(tc, table, w, b, offs, out):
         offsets = held.tile([P, N // 16], U16, name="offsets")
         nc.sync.dma_start(offsets[:], offs)
 
-        table_blocks = []
-        weight_blocks = []
-        for k in range(K_BLOCKS):
-            table_block = held.tile([P, S], BF16, name=f"table{k}")
-            nc.sync.dma_start(table_block[:], table[k * P : (k + 1) * P, :])
-            table_blocks.append(table_block)
-            weight_block = held.tile([P, M], BF16, name=f"weights{k}")
-            nc.scalar.dma_start(weight_block[:], w[k * P : (k + 1) * P, :])
-            weight_blocks.append(weight_block)
-
+        table_blocks = [held.tile([P, S], BF16, name=f"table{k}") for k in range(K_BLOCKS)]
+        weight_blocks = [held.tile([P, M], BF16, name=f"weights{k}") for k in range(K_BLOCKS)]
         bias = held.tile([P, M_BLOCKS], F32, name="bias")
+        nc.scalar.dma_start(table_blocks[0][:], table[0:P, :])
+        nc.sync.dma_start(weight_blocks[0][:], w[0:P, :])
+        nc.scalar.dma_start(weight_blocks[1][:], w[P : 2 * P, :])
+        nc.scalar.dma_start(table_blocks[1][:], table[P : 2 * P, :])
         with nc.allow_non_contiguous_dma(reason="512 bias values, one to a partition"):
-            nc.scalar.dma_start(bias[:], b.rearrange("(a p) o -> p (a o)", p=P))
+            nc.sync.dma_start(bias[:], b.rearrange("(a p) o -> p (a o)", p=P))
 
         zeros = held.tile([P, 1], F32, name="zeros")
         nc.vector.memset(zeros[:], 0.0)
         unused = held.tile([P, 1], F32, name="unused")
         nc.scalar.activation(unused[:], zeros[:], GELU)
-
-        warm_in = held.tile([P, WARM_COLUMNS], BF16, name="warm_in")
-        nc.vector.memset(warm_in[:], 0.0)
-        warm_bank = psum.tile([P, WARM_COLUMNS], F32, name="warm_bank")
-        for i in range(WARM_MATMULS):
-            nc.tensor.matmul(warm_bank[:], warm_in[:, 0:P], warm_in[:], start=True, stop=True)
 
         banks = [psum.tile([P, N], F32, name=f"bank{m}") for m in range(M_BLOCKS)]
         for k in range(K_BLOCKS):

@@ -7,6 +7,7 @@ M = 512
 N = 256
 K_BLOCKS = K // P
 M_BLOCKS = M // P
+SQUARE = 32
 
 FLOPS = 2 * K * M * N
 
@@ -28,13 +29,19 @@ def tile_gather_matmul_kernel(tc, table, w, b, offs, out):
 
         table_blocks = [held.tile([P, S], BF16, name=f"table{k}") for k in range(K_BLOCKS)]
         weight_blocks = [held.tile([P, M], BF16, name=f"weights{k}") for k in range(K_BLOCKS)]
-        bias = held.tile([P, M_BLOCKS], F32, name="bias")
-        nc.scalar.dma_start(table_blocks[0][:], table[0:P, :])
-        nc.sync.dma_start(weight_blocks[0][:], w[0:P, :])
+        for k in range(K_BLOCKS):
+            nc.sync.dma_start(table_blocks[k][:], table[k * P : (k + 1) * P, :])
+
+        bias_rows = held.tile([P, M_BLOCKS * SQUARE], F32, name="bias_rows", align_bytes=64)
+        nc.vector.memset(bias_rows[:], 0.0)
+        nc.scalar.dma_start(weight_blocks[0][:], w[0:P, :])
+        nc.scalar.dma_start(
+            bias_rows[0:P:SQUARE, :].rearrange("q (m p) -> q m p", p=SQUARE),
+            b.rearrange("(m q p) o -> q m (p o)", q=P // SQUARE, p=SQUARE),
+        )
         nc.scalar.dma_start(weight_blocks[1][:], w[P : 2 * P, :])
-        nc.scalar.dma_start(table_blocks[1][:], table[P : 2 * P, :])
-        with nc.allow_non_contiguous_dma(reason="512 bias values, one to a partition"):
-            nc.sync.dma_start(bias[:], b.rearrange("(a p) o -> p (a o)", p=P))
+        bias_columns = held.tile([P, M_BLOCKS * SQUARE], F32, name="bias_columns", align_bytes=64)
+        nc.vector.transpose(bias_columns[:], bias_rows[:])
 
         zeros = held.tile([P, 1], F32, name="zeros")
         nc.vector.memset(zeros[:], 0.0)
@@ -54,5 +61,7 @@ def tile_gather_matmul_kernel(tc, table, w, b, offs, out):
 
         for m in range(M_BLOCKS):
             result = staged.tile([P, N], F32, name="result")
-            nc.scalar.activation(result[:], banks[m][:], GELU, bias=bias[:, m : m + 1])
+            nc.scalar.activation(
+                result[:], banks[m][:], GELU, bias=bias_columns[:, m * SQUARE : m * SQUARE + 1]
+            )
             nc.sync.dma_start(out[m * P : (m + 1) * P, :], result[:])

@@ -31,15 +31,14 @@ def tile_gather_matmul_kernel(tc, table, w, b, offs, out):
         weight_blocks = [held.tile([P, M], BF16, name=f"weights{k}") for k in range(K_BLOCKS)]
         for k in range(K_BLOCKS):
             nc.sync.dma_start(table_blocks[k][:], table[k * P : (k + 1) * P, :])
+            nc.sync.dma_start(weight_blocks[k][:], w[k * P : (k + 1) * P, :])
 
         bias_rows = held.tile([P, M_BLOCKS * SQUARE], F32, name="bias_rows", align_bytes=64)
         nc.vector.memset(bias_rows[:], 0.0)
-        nc.scalar.dma_start(weight_blocks[0][:], w[0:P, :])
         nc.scalar.dma_start(
             bias_rows[0:P:SQUARE, :].rearrange("q (m p) -> q m p", p=SQUARE),
             b.rearrange("(m q p) o -> q m (p o)", q=P // SQUARE, p=SQUARE),
         )
-        nc.scalar.dma_start(weight_blocks[1][:], w[P : 2 * P, :])
         bias_columns = held.tile([P, M_BLOCKS * SQUARE], F32, name="bias_columns", align_bytes=64)
         nc.vector.transpose(bias_columns[:], bias_rows[:])
 

@@ -7,6 +7,7 @@ M = 512
 N = 256
 K_BLOCKS = K // P
 M_BLOCKS = M // P
+M_HALF = M // 2
 SQUARE = 32
 
 FLOPS = 2 * K * M * N
@@ -28,10 +29,16 @@ def tile_gather_matmul_kernel(tc, table, w, b, offs, out):
         nc.sync.dma_start(offsets[:], offs)
 
         table_blocks = [held.tile([P, S], BF16, name=f"table{k}") for k in range(K_BLOCKS)]
-        weight_blocks = [held.tile([P, M], BF16, name=f"weights{k}") for k in range(K_BLOCKS)]
+        weight_halves = [
+            [held.tile([P, M_HALF], BF16, name=f"weights{k}_{h}") for h in range(2)]
+            for k in range(K_BLOCKS)
+        ]
         for k in range(K_BLOCKS):
             nc.sync.dma_start(table_blocks[k][:], table[k * P : (k + 1) * P, :])
-            nc.sync.dma_start(weight_blocks[k][:], w[k * P : (k + 1) * P, :])
+            for h in range(2):
+                nc.sync.dma_start(
+                    weight_halves[k][h][:], w[k * P : (k + 1) * P, h * M_HALF : (h + 1) * M_HALF]
+                )
 
         bias_rows = held.tile([P, M_BLOCKS * SQUARE], F32, name="bias_rows", align_bytes=64)
         nc.vector.memset(bias_rows[:], 0.0)
@@ -50,9 +57,10 @@ def tile_gather_matmul_kernel(tc, table, w, b, offs, out):
         banks = [psum.tile([P, N], F32, name=f"bank{m}") for m in range(M_BLOCKS)]
         for k in range(K_BLOCKS):
             for m in range(M_BLOCKS):
+                half, column = divmod(m * P, M_HALF)
                 nc.tensor.matmul(
                     banks[m][:],
-                    weight_blocks[k][:, m * P : (m + 1) * P],
+                    weight_halves[k][half][:, column : column + P],
                     table_blocks[k][:].indirect(offsets[:]),
                     start=(k == 0),
                     stop=(k == K_BLOCKS - 1),

@@ -22,7 +22,7 @@ def tile_gather_matmul_kernel(tc, table, w, b, offs, out):
     nc = tc.nc
     with (
         tc.tile_pool(name="held", bufs=1) as held,
-        tc.tile_pool(name="staged", bufs=M_BLOCKS) as staged,
+        tc.tile_pool(name="staged", bufs=M_BLOCKS + 1) as staged,
         tc.psum_pool(name="psum", bufs=1) as psum,
     ):
         offsets = held.tile([P, N // 16], U16, name="offsets")
@@ -54,21 +54,24 @@ def tile_gather_matmul_kernel(tc, table, w, b, offs, out):
         unused = held.tile([P, 1], F32, name="unused")
         nc.scalar.activation(unused[:], zeros[:], GELU)
 
-        banks = [psum.tile([P, N], F32, name=f"bank{m}") for m in range(M_BLOCKS)]
+        pieces = [(m, 0, N) for m in range(M_BLOCKS - 1)]
+        pieces += [(M_BLOCKS - 1, first, N // 2) for first in (0, N // 2)]
+
+        banks = [psum.tile([P, count], F32, name=f"bank{i}") for i, (m, first, count) in enumerate(pieces)]
         for k in range(K_BLOCKS):
-            for m in range(M_BLOCKS):
+            for bank, (m, first, count) in zip(banks, pieces):
                 half, column = divmod(m * P, M_HALF)
                 nc.tensor.matmul(
-                    banks[m][:],
+                    bank[:],
                     weight_halves[k][half][:, column : column + P],
-                    table_blocks[k][:].indirect(offsets[:]),
+                    table_blocks[k][:].indirect(offsets[:, first // 16 : (first + count) // 16]),
                     start=(k == 0),
                     stop=(k == K_BLOCKS - 1),
                 )
 
-        for m in range(M_BLOCKS):
-            result = staged.tile([P, N], F32, name="result")
+        for bank, (m, first, count) in zip(banks, pieces):
+            result = staged.tile([P, count], F32, name="result")
             nc.scalar.activation(
-                result[:], banks[m][:], GELU, bias=bias_columns[:, m * SQUARE : m * SQUARE + 1]
+                result[:], bank[:], GELU, bias=bias_columns[:, m * SQUARE : m * SQUARE + 1]
             )
-            nc.sync.dma_start(out[m * P : (m + 1) * P, :], result[:])
+            nc.sync.dma_start(out[m * P : (m + 1) * P, first : first + count], result[:])

@@ -54,8 +54,8 @@ def tile_gather_matmul_kernel(tc, table, w, b, offs, out):
         unused = held.tile([P, 1], F32, name="unused")
         nc.scalar.activation(unused[:], zeros[:], GELU)
 
-        pieces = [(m, 0, N) for m in range(M_BLOCKS - 1)]
-        pieces += [(M_BLOCKS - 1, first, N // 2) for first in (0, N // 2)]
+        pieces = [(0, first, N // 2) for first in (0, N // 2)]
+        pieces += [(m, 0, N) for m in range(1, M_BLOCKS)]
 
         banks = [psum.tile([P, count], F32, name=f"bank{i}") for i, (m, first, count) in enumerate(pieces)]
         for k in range(K_BLOCKS):

@@ -7,7 +7,6 @@ M = 512
 N = 256
 K_BLOCKS = K // P
 M_BLOCKS = M // P
-M_HALF = M // 2
 SQUARE = 32
 
 FLOPS = 2 * K * M * N
@@ -29,16 +28,20 @@ def tile_gather_matmul_kernel(tc, table, w, b, offs, out):
         nc.sync.dma_start(offsets[:], offs)
 
         table_blocks = [held.tile([P, S], BF16, name=f"table{k}") for k in range(K_BLOCKS)]
-        weight_halves = [
-            [held.tile([P, M_HALF], BF16, name=f"weights{k}_{h}") for h in range(2)]
-            for k in range(K_BLOCKS)
-        ]
-        for k in range(K_BLOCKS):
-            nc.sync.dma_start(table_blocks[k][:], table[k * P : (k + 1) * P, :])
-            for h in range(2):
-                nc.sync.dma_start(
-                    weight_halves[k][h][:], w[k * P : (k + 1) * P, h * M_HALF : (h + 1) * M_HALF]
-                )
+        weight_of = {}
+
+        def load_weights(k, first, last):
+            tile = held.tile([P, (last - first) * P], BF16, name=f"weights{k}_{first}")
+            nc.sync.dma_start(tile[:], w[k * P : (k + 1) * P, first * P : last * P])
+            for m in range(first, last):
+                weight_of[k, m] = tile[:, (m - first) * P : (m - first + 1) * P]
+
+        nc.sync.dma_start(table_blocks[0][:], table[0:P, :])
+        load_weights(0, 0, 3)
+        nc.sync.dma_start(table_blocks[1][:], table[P : 2 * P, :])
+        load_weights(1, 0, 2)
+        load_weights(1, 2, 4)
+        load_weights(0, 3, 4)
 
         bias_rows = held.tile([P, M_BLOCKS * SQUARE], F32, name="bias_rows", align_bytes=64)
         nc.vector.memset(bias_rows[:], 0.0)
@@ -60,10 +63,9 @@ def tile_gather_matmul_kernel(tc, table, w, b, offs, out):
         banks = [psum.tile([P, count], F32, name=f"bank{i}") for i, (m, first, count) in enumerate(pieces)]
         for k in range(K_BLOCKS):
             for bank, (m, first, count) in zip(banks, pieces):
-                half, column = divmod(m * P, M_HALF)
                 nc.tensor.matmul(
                     bank[:],
-                    weight_halves[k][half][:, column : column + P],
+                    weight_of[k, m],
                     table_blocks[k][:].indirect(offsets[:, first // 16 : (first + count) // 16]),
                     start=(k == 0),
                     stop=(k == K_BLOCKS - 1),

@@ -36,19 +36,22 @@ def tile_gather_matmul_kernel(tc, table, w, b, offs, out):
             for m in range(first, last):
                 weight_of[k, m] = tile[:, (m - first) * P : (m - first + 1) * P]
 
+        bias_rows = held.tile([P, M_BLOCKS * SQUARE], F32, name="bias_rows", align_bytes=64)
+        nc.vector.memset(bias_rows[:], 0.0)
+
         nc.sync.dma_start(table_blocks[0][:], table[0:P, :])
         load_weights(0, 0, 3)
+
+        nc.sync.dma_start(
+            bias_rows[0:P:SQUARE, :].rearrange("q (m p) -> q m p", p=SQUARE),
+            b.rearrange("(m q p) o -> q m (p o)", q=P // SQUARE, p=SQUARE),
+        )
+
         nc.sync.dma_start(table_blocks[1][:], table[P : 2 * P, :])
         load_weights(1, 0, 2)
         load_weights(1, 2, 4)
         load_weights(0, 3, 4)
 
-        bias_rows = held.tile([P, M_BLOCKS * SQUARE], F32, name="bias_rows", align_bytes=64)
-        nc.vector.memset(bias_rows[:], 0.0)
-        nc.scalar.dma_start(
-            bias_rows[0:P:SQUARE, :].rearrange("q (m p) -> q m p", p=SQUARE),
-            b.rearrange("(m q p) o -> q m (p o)", q=P // SQUARE, p=SQUARE),
-        )
         bias_columns = held.tile([P, M_BLOCKS * SQUARE], F32, name="bias_columns", align_bytes=64)
         nc.vector.transpose(bias_columns[:], bias_rows[:])
 

import concourse.mybir as mybir

P = 128
K = 256
S = 1024
M = 512
N = 256
K_BLOCKS = K // P
M_BLOCKS = M // P
SQUARE = 32

FLOPS = 2 * K * M * N

BF16 = mybir.dt.bfloat16
F32 = mybir.dt.float32
U16 = mybir.dt.uint16
GELU = mybir.ActivationFunctionType.Gelu_apprx_tanh


def tile_gather_matmul_kernel(tc, table, w, b, offs, out):
    nc = tc.nc
    with (
        tc.tile_pool(name="held", bufs=1) as held,
        tc.tile_pool(name="staged", bufs=M_BLOCKS + 1) as staged,
        tc.psum_pool(name="psum", bufs=1) as psum,
    ):
        offsets = held.tile([P, N // 16], U16, name="offsets")
        nc.sync.dma_start(offsets[:], offs)

        table_blocks = [held.tile([P, S], BF16, name=f"table{k}") for k in range(K_BLOCKS)]
        weight_of = {}

        def load_weights(k, first, last):
            tile = held.tile([P, (last - first) * P], BF16, name=f"weights{k}_{first}")
            nc.sync.dma_start(tile[:], w[k * P : (k + 1) * P, first * P : last * P])
            for m in range(first, last):
                weight_of[k, m] = tile[:, (m - first) * P : (m - first + 1) * P]

        bias_rows = held.tile([P, M_BLOCKS * SQUARE], F32, name="bias_rows", align_bytes=64)
        nc.vector.memset(bias_rows[:], 0.0)

        nc.sync.dma_start(table_blocks[0][:], table[0:P, :])
        load_weights(0, 0, 3)

        nc.sync.dma_start(
            bias_rows[0:P:SQUARE, :].rearrange("q (m p) -> q m p", p=SQUARE),
            b.rearrange("(m q p) o -> q m (p o)", q=P // SQUARE, p=SQUARE),
        )

        nc.sync.dma_start(table_blocks[1][:], table[P : 2 * P, :])
        load_weights(1, 0, 2)
        load_weights(1, 2, 4)
        load_weights(0, 3, 4)

        bias_columns = held.tile([P, M_BLOCKS * SQUARE], F32, name="bias_columns", align_bytes=64)
        nc.vector.transpose(bias_columns[:], bias_rows[:])

        zeros = held.tile([P, 1], F32, name="zeros")
        nc.vector.memset(zeros[:], 0.0)
        unused = held.tile([P, 1], F32, name="unused")
        nc.scalar.activation(unused[:], zeros[:], GELU)

        pieces = [(0, first, N // 2) for first in (0, N // 2)]
        pieces += [(m, 0, N) for m in range(1, M_BLOCKS)]

        banks = [psum.tile([P, count], F32, name=f"bank{i}") for i, (m, first, count) in enumerate(pieces)]
        for k in range(K_BLOCKS):
            for bank, (m, first, count) in zip(banks, pieces):
                nc.tensor.matmul(
                    bank[:],
                    weight_of[k, m],
                    table_blocks[k][:].indirect(offsets[:, first // 16 : (first + count) // 16]),
                    start=(k == 0),
                    stop=(k == K_BLOCKS - 1),
                )

        for bank, (m, first, count) in zip(banks, pieces):
            result = staged.tile([P, count], F32, name="result")
            nc.scalar.activation(
                result[:], bank[:], GELU, bias=bias_columns[:, m * SQUARE : m * SQUARE + 1]
            )
            nc.sync.dma_start(out[m * P : (m + 1) * P, first : first + count], result[:])
